import numpy as np
CORES = [0,1,2,3,4,5,6,7,24,25,26,27,28,29,30,31]
N = 16
def setup_inputs(rng):
    return {"x": rng.standard_normal((N, 128, 4096), dtype=np.float32)}
def reference(x):
    s = x.sum(axis=0, dtype=np.float64).astype(x.dtype)
    b = 4096 // N
    return {"y": np.stack([s[:, r * b:(r + 1) * b] for r in range(N)])}

@@ -1,0 +1,65 @@
+import concourse.bass as bass
+import concourse.mybir as mybir
+B = 256
+LF_MASK = 65280
+SCRATCH = {'xs': ('sbuf', [128, 16 * B], 'float32'), 'la': ('sbuf', [128, 7 * B], 'float32'), 'lb': ('sbuf', [128, 7 * B], 'float32'), 'fw': ('sbuf', [128, B], 'float32'), 'cp': ('sbuf', [128, B], 'float32'), 'lp': ('sbuf', [128, B], 'float32')}
+SEMAPHORES = ['ld0', 'ld1', 'arrA', 'arrB', 'arrF', 'arrC', 'arrL', 'sent', 'st1', 'st2']
+GATE = (2, 3, 6, 7)
+
+def blk(t, j):
+    return t[:, j * B:(j + 1) * B]
+
+def rank_program(g, core, T, topo):
+    ch, k = divmod(core, 8)
+    S = T.sem
+
+    def dst_id(c):
+        rid, pid, se = topo.addr(c)
+        return bass.DstId(rid=rid, pnc=pid)
+    if ch in (1, 2):
+        if k not in GATE:
+            return
+        rid, pid, se = topo.addr((24 if ch == 2 else 0) + k - 2)
+        g.wait_ge(S.arrF, 8)
+        g.remote_dma(out_ap=T.cp[:], in_ap=T.fw[:], remote_sem=S.arrC, local_sem=S.sent, pid=pid, routing_id=rid, dma_engine_mask=255)
+        g.wait_ge(S.sent, 8)
+        return
+    base = ch * 8
+    other = 24 - base
+    helper = 16 if ch == 0 else 8
+    loc0 = 0 if ch == 0 else 8
+    rem0 = 8 - loc0
+    sent = 0
+    halves = [(rem0, 0, T.la, S.arrA, S.ld0), (loc0, 1, T.lb, S.arrB, S.ld1)]
+    for b0, flip, land, sem, ld in halves:
+        g.dma_start(out=T.xs[:, b0 * B:(b0 + 8) * B], in_=T.x[:, b0 * B:(b0 + 8) * B]).then_inc(ld, 16)
+    for b0, flip, land, sem, ld in halves:
+        g.wait_ge(ld, 16)
+        trs = []
+        for j in range(8):
+            m = j ^ flip
+            if m == k:
+                continue
+            slot = k if k < m else k - 1
+            trs.append(bass.RemoteDMATransfer(dst_ids=[dst_id(base + m)], dma_engine_mask=3 << 2 * len(trs), remote_sem=sem, src=blk(T.xs, b0 + j), dst=blk(land, slot)))
+        g.remote_dma_fused(trs, local_sem=S.sent)
+        sent += 14
+    g.wait_ge(S.arrA, 14)
+    srcs = [blk(T.la, s) for s in range(7)] + [blk(T.xs, rem0 + k)]
+    if k in GATE:
+        tr = bass.RemoteDMATransfer(dst_ids=[dst_id(other + k)], dma_engine_mask=255, remote_sem=S.arrC, srcs=srcs, dsts=[T.cp[:]], alu_op=1)
+    else:
+        tr = bass.RemoteDMATransfer(dst_ids=[dst_id(helper + k + 2)], dma_engine_mask=255, remote_sem=S.arrF, srcs=srcs, dsts=[T.fw[:]], alu_op=1)
+    g.remote_dma_fused([tr], local_sem=S.sent)
+    sent += 8
+    g.wait_ge(S.arrB, 14)
+    srcs = [blk(T.lb, s) for s in range(7)] + [blk(T.xs, loc0 + (k ^ 1))]
+    g.remote_dma_fused([bass.RemoteDMATransfer(dst_ids=[dst_id(base + (k ^ 1))], dma_engine_mask=LF_MASK, remote_sem=S.arrL, srcs=srcs, dsts=[T.lp[:]], alu_op=1)], local_sem=S.sent)
+    sent += 8
+    g.wait_ge(S.arrL, 8)
+    g.dma_start(out=T.y[:], in_=T.lp[:]).then_inc(S.st1, 16)
+    g.wait_ge(S.st1, 16)
+    g.wait_ge(S.arrC, 8)
+    g.dma_start(out=T.y[:], in_=T.cp[:], accum_op=mybir.AluOpType.add).then_inc(S.st2, 16)
+    g.wait_ge(S.st2, 16)
+    g.wait_ge(S.sent, sent)

@@ -30,10 +30,10 @@ def rank_program(g, core, T, topo):
     loc0 = 0 if ch == 0 else 8
     rem0 = 8 - loc0
     sent = 0
-    halves = [(rem0, 0, T.la, S.arrA, S.ld0), (loc0, 1, T.lb, S.arrB, S.ld1)]
-    for b0, flip, land, sem, ld in halves:
-        g.dma_start(out=T.xs[:, b0 * B:(b0 + 8) * B], in_=T.x[:, b0 * B:(b0 + 8) * B]).then_inc(ld, 16)
-    for b0, flip, land, sem, ld in halves:
+    halves = [(rem0, 0, T.la, S.arrA, S.ld0, g.sync), (loc0, 1, T.lb, S.arrB, S.ld1, g.scalar)]
+    for b0, flip, land, sem, ld, q in halves:
+        q.dma_start(out=T.xs[:, b0 * B:(b0 + 8) * B], in_=T.x[:, b0 * B:(b0 + 8) * B]).then_inc(ld, 16)
+    for b0, flip, land, sem, ld, q in halves:
         g.wait_ge(ld, 16)
         trs = []
         for j in range(8):
@@ -56,8 +56,8 @@ def rank_program(g, core, T, topo):
     srcs = [blk(T.lb, s) for s in range(7)] + [blk(T.xs, loc0 + (k ^ 1))]
     g.remote_dma_fused([bass.RemoteDMATransfer(dst_ids=[dst_id(base + (k ^ 1))], dma_engine_mask=LF_MASK, remote_sem=S.arrL, srcs=srcs, dsts=[T.lp[:]], alu_op=1)], local_sem=S.sent)
     sent += 8
-    g.wait_ge(S.arrL, 8)
-    g.dma_start(out=T.y[:], in_=T.lp[:]).then_inc(S.st1, 16)
+    g.sync.wait_ge(S.arrL, 8)
+    g.sync.dma_start(out=T.y[:], in_=T.lp[:]).then_inc(S.st1, 16)
     g.wait_ge(S.st1, 16)
     g.wait_ge(S.arrC, 8)
     g.dma_start(out=T.y[:], in_=T.cp[:], accum_op=mybir.AluOpType.add).then_inc(S.st2, 16)

@@ -2,8 +2,8 @@ import concourse.bass as bass
 import concourse.mybir as mybir
 B = 256
 LF_MASK = 65280
-SCRATCH = {'xs': ('sbuf', [128, 16 * B], 'float32'), 'la': ('sbuf', [128, 7 * B], 'float32'), 'lb': ('sbuf', [128, 7 * B], 'float32'), 'fw': ('sbuf', [128, B], 'float32'), 'cp': ('sbuf', [128, B], 'float32'), 'lp': ('sbuf', [128, B], 'float32')}
-SEMAPHORES = ['ld0', 'ld1', 'arrA', 'arrB', 'arrF', 'arrC', 'arrL', 'sent', 'st1', 'st2']
+SCRATCH = {'xs': ('sbuf', [128, 16 * B], 'float32'), 'la': ('dram', [8, 128, B], 'float32'), 'lb': ('dram', [8, 128, B], 'float32'), 'fw': ('dram', [128, B], 'float32'), 'cp': ('dram', [128, B], 'float32'), 'lp': ('dram', [128, B], 'float32')}
+SEMAPHORES = ['ld0', 'ld1', 'ow0', 'ow1', 'arrA', 'arrB', 'arrF', 'arrC', 'arrL', 'sent', 'st1', 'st2']
 GATE = (2, 3, 6, 7)
 
 def blk(t, j):
@@ -30,10 +30,12 @@ def rank_program(g, core, T, topo):
     loc0 = 0 if ch == 0 else 8
     rem0 = 8 - loc0
     sent = 0
-    halves = [(rem0, 0, T.la, S.arrA, S.ld0, g.sync), (loc0, 1, T.lb, S.arrB, S.ld1, g.scalar)]
-    for b0, flip, land, sem, ld, q in halves:
+    halves = [(rem0, 0, T.la, S.arrA, S.ld0, S.ow0, g.sync), (loc0, 1, T.lb, S.arrB, S.ld1, S.ow1, g.scalar)]
+    for b0, flip, land, sem, ld, ow, q in halves:
         q.dma_start(out=T.xs[:, b0 * B:(b0 + 8) * B], in_=T.x[:, b0 * B:(b0 + 8) * B]).then_inc(ld, 16)
-    for b0, flip, land, sem, ld, q in halves:
+    for b0, flip, land, sem, ld, ow, q in halves:
+        q.dma_start(out=land[7], in_=blk(T.x, b0 + (k ^ flip))).then_inc(ow, 16)
+    for b0, flip, land, sem, ld, ow, q in halves:
         g.wait_ge(ld, 16)
         trs = []
         for j in range(8):
@@ -41,25 +43,27 @@ def rank_program(g, core, T, topo):
             if m == k:
                 continue
             slot = k if k < m else k - 1
-            trs.append(bass.RemoteDMATransfer(dst_ids=[dst_id(base + m)], dma_engine_mask=3 << 2 * len(trs), remote_sem=sem, src=blk(T.xs, b0 + j), dst=blk(land, slot)))
+            trs.append(bass.RemoteDMATransfer(dst_ids=[dst_id(base + m)], dma_engine_mask=3 << 2 * len(trs), remote_sem=sem, src=blk(T.xs, b0 + j), dst=land[slot]))
         g.remote_dma_fused(trs, local_sem=S.sent)
         sent += 14
+    g.wait_ge(S.ow0, 16)
     g.wait_ge(S.arrA, 14)
-    srcs = [blk(T.la, s) for s in range(7)] + [blk(T.xs, rem0 + k)]
+    srcs = [T.la[s] for s in range(8)]
     if k in GATE:
         tr = bass.RemoteDMATransfer(dst_ids=[dst_id(other + k)], dma_engine_mask=255, remote_sem=S.arrC, srcs=srcs, dsts=[T.cp[:]], alu_op=1)
     else:
         tr = bass.RemoteDMATransfer(dst_ids=[dst_id(helper + k + 2)], dma_engine_mask=255, remote_sem=S.arrF, srcs=srcs, dsts=[T.fw[:]], alu_op=1)
     g.remote_dma_fused([tr], local_sem=S.sent)
     sent += 8
+    g.wait_ge(S.ow1, 16)
     g.wait_ge(S.arrB, 14)
-    srcs = [blk(T.lb, s) for s in range(7)] + [blk(T.xs, loc0 + (k ^ 1))]
+    srcs = [T.lb[s] for s in range(8)]
     g.remote_dma_fused([bass.RemoteDMATransfer(dst_ids=[dst_id(base + (k ^ 1))], dma_engine_mask=LF_MASK, remote_sem=S.arrL, srcs=srcs, dsts=[T.lp[:]], alu_op=1)], local_sem=S.sent)
     sent += 8
     g.sync.wait_ge(S.arrL, 8)
     g.sync.dma_start(out=T.y[:], in_=T.lp[:]).then_inc(S.st1, 16)
     g.wait_ge(S.st1, 16)
     g.wait_ge(S.arrC, 8)
-    g.dma_start(out=T.y[:], in_=T.cp[:], accum_op=mybir.AluOpType.add).then_inc(S.st2, 16)
+    g.dma_start(out=T.y[:], in_=T.cp[:], accum_op=mybir.AluOpType.add, max_dma_last_dim=8192).then_inc(S.st2, 16)
     g.wait_ge(S.st2, 16)
     g.wait_ge(S.sent, sent)

@@ -1,10 +1,11 @@
 import concourse.bass as bass
 import concourse.mybir as mybir
 B = 256
-LF_MASK = 65280
 SCRATCH = {'xs': ('sbuf', [128, 16 * B], 'float32'), 'la': ('dram', [8, 128, B], 'float32'), 'lb': ('dram', [8, 128, B], 'float32'), 'fw': ('dram', [128, B], 'float32'), 'cp': ('dram', [128, B], 'float32'), 'lp': ('dram', [128, B], 'float32')}
 SEMAPHORES = ['ld0', 'ld1', 'ow0', 'ow1', 'arrA', 'arrB', 'arrF', 'arrC', 'arrL', 'sent', 'st1', 'st2']
 GATE = (2, 3, 6, 7)
+ONCHIP = (0, 4)
+VIAHELP = (1, 5)
 
 def blk(t, j):
     return t[:, j * B:(j + 1) * B]
@@ -17,13 +18,14 @@ def rank_program(g, core, T, topo):
         rid, pid, se = topo.addr(c)
         return bass.DstId(rid=rid, pnc=pid)
     if ch in (1, 2):
-        if k not in GATE:
+        if k - 2 not in VIAHELP:
             return
         rid, pid, se = topo.addr((24 if ch == 2 else 0) + k - 2)
         g.wait_ge(S.arrF, 8)
         g.remote_dma(out_ap=T.cp[:], in_ap=T.fw[:], remote_sem=S.arrC, local_sem=S.sent, pid=pid, routing_id=rid, dma_engine_mask=255)
         g.wait_ge(S.sent, 8)
         return
+    gate = k in GATE
     base = ch * 8
     other = 24 - base
     helper = 16 if ch == 0 else 8
@@ -49,21 +51,36 @@ def rank_program(g, core, T, topo):
     g.wait_ge(S.ow0, 16)
     g.wait_ge(S.arrA, 14)
     srcs = [T.la[s] for s in range(8)]
-    if k in GATE:
-        tr = bass.RemoteDMATransfer(dst_ids=[dst_id(other + k)], dma_engine_mask=255, remote_sem=S.arrC, srcs=srcs, dsts=[T.cp[:]], alu_op=1)
+    if gate:
+        tr = bass.RemoteDMATransfer(dst_ids=[dst_id(other + k)], dma_engine_mask=0x00FF, remote_sem=S.arrC, srcs=srcs, dsts=[T.cp[:]], alu_op=1)
+        sent += 8
+    elif k in ONCHIP:
+        tr = bass.RemoteDMATransfer(dst_ids=[dst_id(base + k + 2)], dma_engine_mask=0xFFFF, remote_sem=S.arrF, srcs=srcs, dsts=[T.fw[:]], alu_op=1)
+        sent += 16
     else:
-        tr = bass.RemoteDMATransfer(dst_ids=[dst_id(helper + k + 2)], dma_engine_mask=255, remote_sem=S.arrF, srcs=srcs, dsts=[T.fw[:]], alu_op=1)
+        tr = bass.RemoteDMATransfer(dst_ids=[dst_id(helper + k + 2)], dma_engine_mask=0x00FF, remote_sem=S.arrF, srcs=srcs, dsts=[T.fw[:]], alu_op=1)
+        sent += 8
     g.remote_dma_fused([tr], local_sem=S.sent)
-    sent += 8
     g.wait_ge(S.ow1, 16)
     g.wait_ge(S.arrB, 14)
     srcs = [T.lb[s] for s in range(8)]
-    g.remote_dma_fused([bass.RemoteDMATransfer(dst_ids=[dst_id(base + (k ^ 1))], dma_engine_mask=LF_MASK, remote_sem=S.arrL, srcs=srcs, dsts=[T.lp[:]], alu_op=1)], local_sem=S.sent)
-    sent += 8
-    g.sync.wait_ge(S.arrL, 8)
-    g.sync.dma_start(out=T.y[:], in_=T.lp[:]).then_inc(S.st1, 16)
+    nl = 16 if k in ONCHIP else 8
+    nl_in = 16 if (k ^ 1) in ONCHIP else 8
+    g.remote_dma_fused([bass.RemoteDMATransfer(dst_ids=[dst_id(base + (k ^ 1))], dma_engine_mask=0xFFFF if nl == 16 else 0xFF00, remote_sem=S.arrL, srcs=srcs, dsts=[T.lp[:]], alu_op=1)], local_sem=S.sent)
+    sent += nl
+    if gate and k - 2 in ONCHIP:
+        rid, pid, se = topo.addr(other + k - 2)
+        g.wait_ge(S.arrF, 16)
+        g.remote_dma(out_ap=T.cp[:], in_ap=T.fw[:], remote_sem=S.arrC, local_sem=S.sent, pid=pid, routing_id=rid, dma_engine_mask=0x00FF)
+        sent += 8
+    if gate:
+        first, second = (S.arrC, 8, T.cp), (S.arrL, nl_in, T.lp)
+    else:
+        first, second = (S.arrL, nl_in, T.lp), (S.arrC, 8, T.cp)
+    g.sync.wait_ge(first[0], first[1])
+    g.sync.dma_start(out=T.y[:], in_=first[2][:]).then_inc(S.st1, 16)
     g.wait_ge(S.st1, 16)
-    g.wait_ge(S.arrC, 8)
-    g.dma_start(out=T.y[:], in_=T.cp[:], accum_op=mybir.AluOpType.add, max_dma_last_dim=8192).then_inc(S.st2, 16)
+    g.wait_ge(second[0], second[1])
+    g.dma_start(out=T.y[:], in_=second[2][:], accum_op=mybir.AluOpType.add, max_dma_last_dim=8192).then_inc(S.st2, 16)
     g.wait_ge(S.st2, 16)
     g.wait_ge(S.sent, sent)

import concourse.bass as bass
import concourse.mybir as mybir
B = 256
SCRATCH = {'xs': ('sbuf', [128, 16 * B], 'float32'), 'la': ('dram', [8, 128, B], 'float32'), 'lb': ('dram', [8, 128, B], 'float32'), 'fw': ('dram', [128, B], 'float32'), 'cp': ('dram', [128, B], 'float32'), 'lp': ('dram', [128, B], 'float32')}
SEMAPHORES = ['ld0', 'ld1', 'ow0', 'ow1', 'arrA', 'arrB', 'arrF', 'arrC', 'arrL', 'sent', 'st1', 'st2']
GATE = (2, 3, 6, 7)
ONCHIP = (0, 4)
VIAHELP = (1, 5)

def blk(t, j):
    return t[:, j * B:(j + 1) * B]

def rank_program(g, core, T, topo):
    ch, k = divmod(core, 8)
    S = T.sem

    def dst_id(c):
        rid, pid, se = topo.addr(c)
        return bass.DstId(rid=rid, pnc=pid)
    if ch in (1, 2):
        if k - 2 not in VIAHELP:
            return
        rid, pid, se = topo.addr((24 if ch == 2 else 0) + k - 2)
        g.wait_ge(S.arrF, 8)
        g.remote_dma(out_ap=T.cp[:], in_ap=T.fw[:], remote_sem=S.arrC, local_sem=S.sent, pid=pid, routing_id=rid, dma_engine_mask=255)
        g.wait_ge(S.sent, 8)
        return
    gate = k in GATE
    base = ch * 8
    other = 24 - base
    helper = 16 if ch == 0 else 8
    loc0 = 0 if ch == 0 else 8
    rem0 = 8 - loc0
    sent = 0
    halves = [(rem0, 0, T.la, S.arrA, S.ld0, S.ow0, g.sync), (loc0, 1, T.lb, S.arrB, S.ld1, S.ow1, g.scalar)]
    for b0, flip, land, sem, ld, ow, q in halves:
        q.dma_start(out=T.xs[:, b0 * B:(b0 + 8) * B], in_=T.x[:, b0 * B:(b0 + 8) * B]).then_inc(ld, 16)
    for b0, flip, land, sem, ld, ow, q in halves:
        q.dma_start(out=land[7], in_=blk(T.x, b0 + (k ^ flip))).then_inc(ow, 16)
    for b0, flip, land, sem, ld, ow, q in halves:
        g.wait_ge(ld, 16)
        trs = []
        for j in range(8):
            m = j ^ flip
            if m == k:
                continue
            slot = k if k < m else k - 1
            trs.append(bass.RemoteDMATransfer(dst_ids=[dst_id(base + m)], dma_engine_mask=3 << 2 * len(trs), remote_sem=sem, src=blk(T.xs, b0 + j), dst=land[slot]))
        g.remote_dma_fused(trs, local_sem=S.sent)
        sent += 14
    g.wait_ge(S.ow0, 16)
    g.wait_ge(S.arrA, 14)
    srcs = [T.la[s] for s in range(8)]
    if gate:
        tr = bass.RemoteDMATransfer(dst_ids=[dst_id(other + k)], dma_engine_mask=0x00FF, remote_sem=S.arrC, srcs=srcs, dsts=[T.cp[:]], alu_op=1)
        sent += 8
    elif k in ONCHIP:
        tr = bass.RemoteDMATransfer(dst_ids=[dst_id(base + k + 2)], dma_engine_mask=0xFFFF, remote_sem=S.arrF, srcs=srcs, dsts=[T.fw[:]], alu_op=1)
        sent += 16
    else:
        tr = bass.RemoteDMATransfer(dst_ids=[dst_id(helper + k + 2)], dma_engine_mask=0x00FF, remote_sem=S.arrF, srcs=srcs, dsts=[T.fw[:]], alu_op=1)
        sent += 8
    g.remote_dma_fused([tr], local_sem=S.sent)
    g.wait_ge(S.ow1, 16)
    g.wait_ge(S.arrB, 14)
    srcs = [T.lb[s] for s in range(8)]
    nl = 16 if k in ONCHIP else 8
    nl_in = 16 if (k ^ 1) in ONCHIP else 8
    g.remote_dma_fused([bass.RemoteDMATransfer(dst_ids=[dst_id(base + (k ^ 1))], dma_engine_mask=0xFFFF if nl == 16 else 0xFF00, remote_sem=S.arrL, srcs=srcs, dsts=[T.lp[:]], alu_op=1)], local_sem=S.sent)
    sent += nl
    if gate and k - 2 in ONCHIP:
        rid, pid, se = topo.addr(other + k - 2)
        g.wait_ge(S.arrF, 16)
        g.remote_dma(out_ap=T.cp[:], in_ap=T.fw[:], remote_sem=S.arrC, local_sem=S.sent, pid=pid, routing_id=rid, dma_engine_mask=0x00FF)
        sent += 8
    if gate:
        first, second = (S.arrC, 8, T.cp), (S.arrL, nl_in, T.lp)
    else:
        first, second = (S.arrL, nl_in, T.lp), (S.arrC, 8, T.cp)
    g.sync.wait_ge(first[0], first[1])
    g.sync.dma_start(out=T.y[:], in_=first[2][:]).then_inc(S.st1, 16)
    g.wait_ge(S.st1, 16)
    g.wait_ge(second[0], second[1])
    g.dma_start(out=T.y[:], in_=second[2][:], accum_op=mybir.AluOpType.add, max_dma_last_dim=8192).then_inc(S.st2, 16)
    g.wait_ge(S.st2, 16)
    g.wait_ge(S.sent, sent)
